import numpy as np, ml_dtypes
CORES = [2,3,42,43,82,83,122,123]
N = 8
S, B = 3, 128
def setup_inputs(rng):
    a = (rng.standard_normal((128, 128), dtype=np.float32) / 12).astype(ml_dtypes.bfloat16)
    return {"x": rng.standard_normal((N, 128, S * B), dtype=np.float32).astype(ml_dtypes.bfloat16), "a": np.broadcast_to(a, (N, 128, 128)).copy(), "at": np.broadcast_to(a.T, (N, 128, 128)).copy()}
def setup_inputs_big(rng):
    d = setup_inputs(rng)
    for k in ("x",): d[k] = (d[k].astype(np.float32) * 1048576.0).astype(d[k].dtype)
    return d
def setup_inputs_small(rng):
    d = setup_inputs(rng)
    for k in ("x",): d[k] = (d[k].astype(np.float32) * (1 / 1048576.0)).astype(d[k].dtype)
    return d
def setup_inputs_apart(rng):
    d = setup_inputs(rng)
    f = (10.0 ** rng.permutation(np.linspace(-1.5, 1.5, N))).astype(np.float32).reshape(N, 1, 1)
    for k in ("x",): d[k] = (d[k].astype(np.float32) * f).astype(d[k].dtype)
    return d
def reference(x, a, at):
    X, A = x.astype(np.float64), a.astype(np.float64)
    y = np.zeros((N, 128, S * B)); h = np.zeros((128, B))
    for r in range(N):
        for s in range(S):
            h = A[r].T @ h + X[r][:, B * s:B * s + B]
            y[r][:, B * s:B * s + B] = h
    return {"y": y.astype(ml_dtypes.bfloat16)}

@@ -1,0 +1,270 @@
+from concourse.bass import DstId, RemoteDMATransfer
+from concourse.mybir import AluOpType
+
+N, S, B = 8, 3, 128
+SPAN = 1
+NSLOT = N - 1 + N // 2 - 1
+
+AT, A1, A2, A3, Q3, A6, Q6, Q12 = 0, 1, 2, 3, 4, 7, 8, 12
+TRI = [1, 5, 9, 13, 16, 19, 22]
+NW = 25
+JOBS = [
+    ("j1", [("a2", 2, 1, AT, A1)]),
+    ("j2", [("a3", 3, 1, AT, A2), ("q3", 4, 1, A2, AT)]),
+    ("j3", [("t1", 5, 3, Q3, A1), ("q6", 8, 1, A3, Q3)]),
+    ("j4a", [("t2", 9, 3, Q6, A1), ("q12", 12, 1, A6, Q6)]),
+    ("j4b", [("t3", 13, 3, Q6, 5)]),
+    ("j5a", [("t4", 16, 3, Q12, 1)]),
+    ("j5b", [("t5", 19, 3, Q12, 5)]),
+    ("j5c", [("t6", 22, 3, Q12, 9)]),
+]
+DEPS = {"a": [], "at": [], "a2": ["a", "at"], "a3": ["at", "a2"], "q3": ["a2", "at"], "t1": ["q3", "a", "a2", "a3"],
+        "q6": ["a3", "q3"], "t2": ["q6", "a", "a2", "a3"], "q12": ["t1", "q6"], "t3": ["q6", "t1"],
+        "t4": ["q12", "a", "a2", "a3"], "t5": ["q12", "t1"], "t6": ["q12", "t2"]}
+ITEM_JOB = {}
+for _j, _parts in JOBS:
+    for _p in _parts:
+        ITEM_JOB[_p[0]] = _j
+
+SCRATCH = {
+    "xs": ("sbuf", [128, S * B], "bfloat16"),
+    "w": ("sbuf", [128, NW * B], "bfloat16"),
+    "lc": ("sbuf", [128, 2 * B], "bfloat16"),
+    "dd": ("sbuf", [128, B], "bfloat16"),
+    "land": ("sbuf", [128, NSLOT * B], "bfloat16"),
+    "ys": ("sbuf", [128, S * B], "bfloat16"),
+    "pc": ("psum", [128, 512], "float32"),
+    "py0": ("psum", [128, 512], "float32"),
+    "py1": ("psum", [128, 512], "float32"),
+    "py2": ("psum", [128, 512], "float32"),
+    "pp0": ("psum", [128, 512], "float32"),
+    "pp1": ("psum", [128, 512], "float32"),
+    "pp2": ("psum", [128, 512], "float32"),
+}
+SEMAPHORES = (["ldx", "lda", "ldat", "mm1", "l1", "mm2", "c", "dm", "d", "y0", "y1", "y2", "fin", "st", "sent"]
+              + ["m%d" % i for i in range(NSLOT)]
+              + ["t" + j for j, _ in JOBS] + ["v" + j for j, _ in JOBS])
+
+
+def _bits(m):
+    return bin(m).count("1")
+
+
+def rank_program(g, core, T, topo):
+    r = T.rank_of(core)
+    if r is None:
+        return
+    cores = list(T.cores)
+    groups = []
+    for i, c in enumerate(cores):
+        if groups and topo.chip(cores[groups[-1][0]]) == topo.chip(c):
+            groups[-1].append(i)
+        else:
+            groups.append([i])
+    G = len(groups)
+    grp = {q: k for k, m in enumerate(groups) for q in m}
+    k = grp[r]
+    p = groups[k].index(r)
+    PE, V, SY, SC = g.tensor, g.vector, g.sync, g.scalar
+
+    def direct_groups(kk):
+        return [m for m in range(kk + 1, G) if m - kk <= SPAN]
+
+    def comb_groups(kk):
+        return [m for m in range(kk + 1, G) if m - kk > SPAN]
+
+    def off_mask(q):
+        m = None
+        for o in range(N):
+            if grp[o] != grp[q]:
+                mm = topo.mask(cores[q], cores[o])
+                m = mm if m is None else (m & mm)
+        return m
+
+    def swap_mask(q):
+        mate = [o for o in groups[grp[q]] if o != q][0]
+        on, off = topo.mask(cores[q], cores[mate]), off_mask(q)
+        if direct_groups(grp[q]) and not comb_groups(grp[q]) and (on & ~off):
+            return on & ~off
+        return on & off
+
+    seen = {}
+
+    def wait(q, qn, sem, val):
+        if seen.get((qn, sem), 0) >= val:
+            return
+        seen[(qn, sem)] = val
+        q.wait_ge(T.sem[sem], val)
+
+    def ready(q, qn, item):
+        if item == "a":
+            wait(q, qn, "lda", 16)
+        elif item == "at":
+            wait(q, qn, "ldat", 16)
+        else:
+            wait(q, qn, "v" + ITEM_JOB[item], 1)
+
+    def blk(t, i, n=1):
+        return t[:, i * B:(i + n) * B]
+
+    msgs = []
+    if p == 1:
+        msgs.append((r - 1, 0, _bits(swap_mask(r - 1))))
+    for kk in range(k - 1, -1, -1):
+        if k - kk <= SPAN:
+            for q in reversed(groups[kk]):
+                msgs.append((q, r - q - 1, _bits(off_mask(q))))
+    for kk in range(k - 1, -1, -1):
+        if k - kk > SPAN:
+            msgs.append((N - 1 + kk, r - groups[kk][-1] - 1, _bits(off_mask(groups[kk][p]))))
+    make_d = bool(comb_groups(k))
+
+    need = set()
+
+    def want(item):
+        if item in need:
+            return
+        need.add(item)
+        for d in DEPS[item]:
+            want(d)
+    want("a")
+    for _, m, _e in msgs:
+        if m == 0:
+            want("a2")
+            want("a3")
+        else:
+            want("t%d" % m)
+    if make_d:
+        want("a3")
+    jobs = []
+    for name, parts in JOBS:
+        ps = [q for q in parts if q[0] in need]
+        if ps:
+            jobs.append((name, ps))
+
+    SY.dma_start(T.xs[:, :], T.x[:, :]).then_inc(T.sem.ldx, 16)
+    SC.dma_start(blk(T.w, A1), T.a[:, :]).then_inc(T.sem.lda, 16)
+    if "at" in need:
+        SC.dma_start(blk(T.w, AT), T.at[:, :]).then_inc(T.sem.ldat, 16)
+
+    banks = [T.pp0, T.pp1, T.pp2]
+
+    def job_pe(i):
+        name, ps = jobs[i]
+        if i >= len(banks):
+            wait(PE, "pe", "v" + jobs[i - len(banks)][0], 1)
+        col = 0
+        for item, _o, n, lh, rh in ps:
+            for d in DEPS[item]:
+                ready(PE, "pe", d)
+            PE.matmul(banks[i % len(banks)][:, col * B:(col + n) * B], blk(T.w, lh), blk(T.w, rh, n),
+                      start=True, stop=True).then_inc(T.sem["t" + name], 1)
+            col += n
+
+    def job_v(i):
+        name, ps = jobs[i]
+        n = sum(q[2] for q in ps)
+        wait(V, "v", "t" + name, len(ps))
+        V.tensor_copy(blk(T.w, ps[0][1], n), banks[i % len(banks)][:, 0:n * B]).then_inc(T.sem["v" + name], 1)
+
+    early = [i for i, j in enumerate(jobs) if j[0] in ("j1", "j2")]
+    late = [i for i, j in enumerate(jobs) if j[0] not in ("j1", "j2")]
+
+    wait(PE, "pe", "lda", 16)
+    wait(PE, "pe", "ldx", 16)
+    PE.matmul(blk(T.pc, 0), blk(T.w, A1), blk(T.xs, 0), start=True, stop=True).then_inc(T.sem.mm1, 1)
+    if early:
+        job_pe(early[0])
+    wait(PE, "pe", "l1", 1)
+    PE.matmul(blk(T.pc, 1), blk(T.w, A1), blk(T.lc, 0), start=True, stop=True).then_inc(T.sem.mm2, 1)
+    for i in early[1:]:
+        job_pe(i)
+    if make_d:
+        ready(PE, "pe", "a3")
+        wait(PE, "pe", "c", 1)
+        if p == 0:
+            first = blk(T.lc, 1)
+        else:
+            wait(PE, "pe", "m%d" % (r - 1), _bits(swap_mask(r - 1)))
+            first = blk(T.land, r - 1)
+        PE.matmul(blk(T.pc, 2), blk(T.w, A3), first, start=True, stop=True).then_inc(T.sem.dm, 1)
+    for i in late:
+        job_pe(i)
+    py = [T.py0, T.py1, T.py2]
+    for j, (slot, m, ne) in enumerate(msgs):
+        wait(PE, "pe", "m%d" % slot, ne)
+        for s in range(S):
+            ready(PE, "pe", ("a", "a2", "a3")[s] if m == 0 else "t%d" % m)
+            PE.matmul(blk(py[s], 0), blk(T.w, TRI[m] + s), blk(T.land, slot),
+                      start=(j == 0), stop=(j == len(msgs) - 1)).then_inc(T.sem["y%d" % s], 1)
+
+    wait(V, "v", "ldx", 16)
+    wait(V, "v", "mm1", 1)
+    V.tensor_tensor(blk(T.lc, 0), blk(T.pc, 0), blk(T.xs, 1), op=AluOpType.add).then_inc(T.sem.l1, 1)
+    wait(V, "v", "mm2", 1)
+    V.tensor_tensor(blk(T.lc, 1), blk(T.pc, 1), blk(T.xs, 2), op=AluOpType.add).then_inc(T.sem.c, 1)
+    for i in early:
+        job_v(i)
+    if make_d:
+        wait(V, "v", "dm", 1)
+        if p == 0:
+            wait(V, "v", "m%d" % (r + 1), _bits(swap_mask(r + 1)))
+            second = blk(T.land, r + 1)
+        else:
+            wait(V, "v", "c", 1)
+            second = blk(T.lc, 1)
+        V.tensor_tensor(T.dd[:, :], blk(T.pc, 2), second, op=AluOpType.add).then_inc(T.sem.d, 1)
+    for i in late:
+        job_v(i)
+    if msgs:
+        wait(V, "v", "l1", 1)
+        wait(V, "v", "c", 1)
+        loc = [blk(T.xs, 0), blk(T.lc, 0), blk(T.lc, 1)]
+        for s in range(S):
+            wait(V, "v", "y%d" % s, len(msgs))
+            V.tensor_tensor(blk(T.ys, s), blk(py[s], 0), loc[s], op=AluOpType.add).then_inc(T.sem.fin, 1)
+
+    sent = [0]
+
+    def send(src, slot, dests, mask):
+        for o in dests:
+            if not topo.may_write(core, cores[o]):
+                raise ValueError("rank %d may not write to rank %d" % (r, o))
+        ids = [topo.addr(cores[o]) for o in dests]
+        if len(dests) == 1:
+            g.remote_dma(out_ap=blk(T.land, slot), in_ap=src, remote_sem=T.sem["m%d" % slot], local_sem=T.sem.sent,
+                         pid=ids[0][1], routing_id=ids[0][0], dma_engine_mask=mask)
+        else:
+            g.remote_dma_fused([RemoteDMATransfer(dst_ids=[DstId(rid=a[0], pnc=a[1]) for a in ids], dma_engine_mask=mask,
+                                                  remote_sem=T.sem["m%d" % slot], srcs=[src],
+                                                  dsts=[blk(T.land, slot) for _ in ids], alu_op=0)], local_sem=T.sem.sent)
+        sent[0] += _bits(mask)
+
+    direct = [o for m in direct_groups(k) for o in groups[m]]
+    swap = p == 0 or make_d
+    mate = [o for o in groups[k] if o != r][0]
+    if swap or direct:
+        wait(g, "g", "c", 1)
+    if swap and make_d:
+        send(blk(T.lc, 1), r, [mate], swap_mask(r))
+    if direct:
+        send(blk(T.lc, 1), r, direct, off_mask(r))
+    if swap and not make_d:
+        send(blk(T.lc, 1), r, [mate], swap_mask(r))
+    if make_d:
+        wait(g, "g", "d", 1)
+        send(T.dd[:, :], N - 1 + k, [groups[m][p] for m in comb_groups(k)], off_mask(r))
+    if sent[0]:
+        wait(g, "g", "sent", sent[0])
+
+    if msgs:
+        wait(SY, "sy", "fin", S)
+        SY.dma_start(T.y[:, :], T.ys[:, :]).then_inc(T.sem.st, 16)
+        wait(SY, "sy", "st", 16)
+    else:
+        wait(SY, "sy", "ldx", 16)
+        SY.dma_start(T.y[:, 0:B], blk(T.xs, 0)).then_inc(T.sem.st, 16)
+        wait(SY, "sy", "l1", 1)
+        wait(SY, "sy", "c", 1)
+        SY.dma_start(T.y[:, B:S * B], T.lc[:, :]).then_inc(T.sem.st, 16)
+        wait(SY, "sy", "st", 32)

@@ -1,39 +1,43 @@
 from concourse.bass import DstId, RemoteDMATransfer
-from concourse.mybir import AluOpType
+from concourse.mybir import AluOpType, ActivationFunctionType
 
 N, S, B = 8, 3, 128
 SPAN = 1
 NSLOT = N - 1 + N // 2 - 1
 
-AT, A1, A2, A3, Q3, A6, Q6, Q12 = 0, 1, 2, 3, 4, 7, 8, 12
-TRI = [1, 5, 9, 13, 16, 19, 22]
-NW = 25
+AT, A1, A2, A3, A4, A5, A6, Q6, Q3, Q12 = 0, 1, 2, 3, 4, 5, 6, 7, 8, 12
+TRI = [1, 4, 9, 13, 16, 19]
+NW = 22
 JOBS = [
-    ("j1", [("a2", 2, 1, AT, A1)]),
-    ("j2", [("a3", 3, 1, AT, A2), ("q3", 4, 1, A2, AT)]),
-    ("j3", [("t1", 5, 3, Q3, A1), ("q6", 8, 1, A3, Q3)]),
-    ("j4a", [("t2", 9, 3, Q6, A1), ("q12", 12, 1, A6, Q6)]),
-    ("j4b", [("t3", 13, 3, Q6, 5)]),
-    ("j5a", [("t4", 16, 3, Q12, 1)]),
-    ("j5b", [("t5", 19, 3, Q12, 5)]),
-    ("j5c", [("t6", 22, 3, Q12, 9)]),
+    ("j1", "s", [("a2", 2, 1, AT, A1)]),
+    ("j2q", "s", [("q3", 8, 1, A2, AT)]),
+    ("j2a", "v", [("a3", 3, 1, AT, A2)]),
+    ("j3a", "s", [("a45", 4, 2, Q3, A1)]),
+    ("j3b", "v", [("a6", 6, 1, Q3, A3), ("q6", 7, 1, A3, Q3)]),
+    ("j4a", "s", [("t2", 9, 3, Q6, A1), ("q12", 12, 1, A6, Q6)]),
+    ("j4b", "v", [("t3", 13, 3, Q6, A4)]),
+    ("j5a", "v", [("t4", 16, 3, Q12, A1)]),
+    ("j5b", "s", [("t5", 19, 3, Q12, A4)]),
 ]
-DEPS = {"a": [], "at": [], "a2": ["a", "at"], "a3": ["at", "a2"], "q3": ["a2", "at"], "t1": ["q3", "a", "a2", "a3"],
-        "q6": ["a3", "q3"], "t2": ["q6", "a", "a2", "a3"], "q12": ["t1", "q6"], "t3": ["q6", "t1"],
-        "t4": ["q12", "a", "a2", "a3"], "t5": ["q12", "t1"], "t6": ["q12", "t2"]}
+DEPS = {"a": [], "at": [], "a2": ["a", "at"], "a3": ["at", "a2"], "q3": ["a2", "at"], "a45": ["q3", "a", "a2"],
+        "a6": ["q3", "a3"], "q6": ["a3", "q3"], "t2": ["q6", "a", "a2", "a3"], "q12": ["a6", "q6"],
+        "t3": ["q6", "a45", "a6"], "t4": ["q12", "a", "a2", "a3"], "t5": ["q12", "a45", "a6"]}
 ITEM_JOB = {}
-for _j, _parts in JOBS:
+for _j, _e, _parts in JOBS:
     for _p in _parts:
         ITEM_JOB[_p[0]] = _j
 
 SCRATCH = {
     "xs": ("sbuf", [128, S * B], "bfloat16"),
+    "xm": ("sbuf", [128, S * B], "bfloat16"),
     "w": ("sbuf", [128, NW * B], "bfloat16"),
     "lc": ("sbuf", [128, 2 * B], "bfloat16"),
+    "cf": ("sbuf", [128, B], "bfloat16"),
     "dd": ("sbuf", [128, B], "bfloat16"),
     "land": ("sbuf", [128, NSLOT * B], "bfloat16"),
     "ys": ("sbuf", [128, S * B], "bfloat16"),
     "pc": ("psum", [128, 512], "float32"),
+    "pd": ("psum", [128, 512], "float32"),
     "py0": ("psum", [128, 512], "float32"),
     "py1": ("psum", [128, 512], "float32"),
     "py2": ("psum", [128, 512], "float32"),
@@ -41,13 +45,22 @@ SCRATCH = {
     "pp1": ("psum", [128, 512], "float32"),
     "pp2": ("psum", [128, 512], "float32"),
 }
-SEMAPHORES = (["ldx", "lda", "ldat", "mm1", "l1", "mm2", "c", "dm", "d", "y0", "y1", "y2", "fin", "st", "sent"]
+SEMAPHORES = (["ldx", "lda", "ldat", "mm1", "l1", "mm2", "c", "dm", "d", "cm", "cfs", "mx", "y0", "y1", "y2", "fin", "st",
+               "sent"]
               + ["m%d" % i for i in range(NSLOT)]
-              + ["t" + j for j, _ in JOBS] + ["v" + j for j, _ in JOBS])
+              + ["t" + j[0] for j in JOBS] + ["v" + j[0] for j in JOBS])
 
 
 def _bits(m):
     return bin(m).count("1")
+
+
+def _tri_items(m):
+    if m == 0:
+        return ["a", "a2", "a3"]
+    if m == 1:
+        return ["a45", "a6"]
+    return ["t%d" % m]
 
 
 def rank_program(g, core, T, topo):
@@ -81,13 +94,6 @@ def rank_program(g, core, T, topo):
                 m = mm if m is None else (m & mm)
         return m
 
-    def swap_mask(q):
-        mate = [o for o in groups[grp[q]] if o != q][0]
-        on, off = topo.mask(cores[q], cores[mate]), off_mask(q)
-        if direct_groups(grp[q]) and not comb_groups(grp[q]) and (on & ~off):
-            return on & ~off
-        return on & off
-
     seen = {}
 
     def wait(q, qn, sem, val):
@@ -107,40 +113,58 @@ def rank_program(g, core, T, topo):
     def blk(t, i, n=1):
         return t[:, i * B:(i + n) * B]
 
+    mate = [o for o in groups[k] if o != r][0]
+    make_d = bool(comb_groups(k))
+    send_x = p == 0 or make_d
+    recv_x = p == 1 or make_d
+    nx = _bits(topo.mask(cores[mate], core))
+
     msgs = []
     if p == 1:
-        msgs.append((r - 1, 0, _bits(swap_mask(r - 1))))
+        msgs.append((T.cf[:, :], 0, "cfs", 1))
     for kk in range(k - 1, -1, -1):
         if k - kk <= SPAN:
             for q in reversed(groups[kk]):
-                msgs.append((q, r - q - 1, _bits(off_mask(q))))
+                msgs.append((blk(T.land, q), r - q - 1, "m%d" % q, _bits(off_mask(q))))
     for kk in range(k - 1, -1, -1):
         if k - kk > SPAN:
-            msgs.append((N - 1 + kk, r - groups[kk][-1] - 1, _bits(off_mask(groups[kk][p]))))
-    make_d = bool(comb_groups(k))
+            msgs.append((blk(T.land, N - 1 + kk), r - groups[kk][-1] - 1, "m%d" % (N - 1 + kk),
+                         _bits(off_mask(groups[kk][p]))))
 
-    need = set()
+    def closure(items):
+        out = set()
 
-    def want(item):
-        if item in need:
-            return
-        need.add(item)
-        for d in DEPS[item]:
-            want(d)
-    want("a")
-    for _, m, _e in msgs:
-        if m == 0:
-            want("a2")
-            want("a3")
-        else:
-            want("t%d" % m)
+        def want(item):
+            if item in out:
+                return
+            out.add(item)
+            for d in DEPS[item]:
+                want(d)
+        for it in items:
+            want(it)
+        return out
+
+    dneed = []
     if make_d:
-        want("a3")
-    jobs = []
-    for name, parts in JOBS:
+        dneed = ["a", "a2", "a3"] if p == 0 else ["a3", "a45"]
+    wanted = ["a"] + dneed
+    if p == 1:
+        wanted += ["a", "a2"]
+    for _src, m, _s, _n in msgs:
+        wanted += _tri_items(m)
+    need = closure(wanted)
+    first = closure(dneed) if make_d else need
+    early, late = [], []
+    for name, eng, parts in JOBS:
         ps = [q for q in parts if q[0] in need]
-        if ps:
-            jobs.append((name, ps))
+        if not ps:
+            continue
+        if any(q[0] in first for q in ps):
+            early.append((name, eng, ps))
+        else:
+            late.append((name, eng, ps))
+    jobs = early + late
+    pos = {j[0]: i for i, j in enumerate(jobs)}
 
     SY.dma_start(T.xs[:, :], T.x[:, :]).then_inc(T.sem.ldx, 16)
     SC.dma_start(blk(T.w, A1), T.a[:, :]).then_inc(T.sem.lda, 16)
@@ -149,8 +173,9 @@ def rank_program(g, core, T, topo):
 
     banks = [T.pp0, T.pp1, T.pp2]
 
-    def job_pe(i):
-        name, ps = jobs[i]
+    def job_pe(job):
+        name, _eng, ps = job
+        i = pos[name]
         if i >= len(banks):
             wait(PE, "pe", "v" + jobs[i - len(banks)][0], 1)
         col = 0
@@ -161,14 +186,17 @@ def rank_program(g, core, T, topo):
                       start=True, stop=True).then_inc(T.sem["t" + name], 1)
             col += n
 
-    def job_v(i):
-        name, ps = jobs[i]
+    def job_copy(job):
+        name, eng, ps = job
+        i = pos[name]
         n = sum(q[2] for q in ps)
-        wait(V, "v", "t" + name, len(ps))
-        V.tensor_copy(blk(T.w, ps[0][1], n), banks[i % len(banks)][:, 0:n * B]).then_inc(T.sem["v" + name], 1)
-
-    early = [i for i, j in enumerate(jobs) if j[0] in ("j1", "j2")]
-    late = [i for i, j in enumerate(jobs) if j[0] not in ("j1", "j2")]
+        out, src = blk(T.w, ps[0][1], n), banks[i % len(banks)][:, 0:n * B]
+        if eng == "v":
+            wait(V, "v", "t" + name, len(ps))
+            V.tensor_copy(out, src).then_inc(T.sem["v" + name], 1)
+        else:
+            wait(SC, "sc", "t" + name, len(ps))
+            SC.activation(out, src, ActivationFunctionType.Copy).then_inc(T.sem["v" + name], 1)
 
     wait(PE, "pe", "lda", 16)
     wait(PE, "pe", "ldx", 16)
@@ -177,25 +205,34 @@ def rank_program(g, core, T, topo):
         job_pe(early[0])
     wait(PE, "pe", "l1", 1)
     PE.matmul(blk(T.pc, 1), blk(T.w, A1), blk(T.lc, 0), start=True, stop=True).then_inc(T.sem.mm2, 1)
-    for i in early[1:]:
-        job_pe(i)
+    for j in early[1:]:
+        job_pe(j)
     if make_d:
-        ready(PE, "pe", "a3")
-        wait(PE, "pe", "c", 1)
         if p == 0:
-            first = blk(T.lc, 1)
+            terms = [(A3, blk(T.lc, 1), "a3"), (A1, blk(T.xm, 1), "a"), (A2, blk(T.xm, 0), "a2")]
+            wait(PE, "pe", "c", 1)
         else:
-            wait(PE, "pe", "m%d" % (r - 1), _bits(swap_mask(r - 1)))
-            first = blk(T.land, r - 1)
-        PE.matmul(blk(T.pc, 2), blk(T.w, A3), first, start=True, stop=True).then_inc(T.sem.dm, 1)
-    for i in late:
-        job_pe(i)
+            terms = [(A3, blk(T.xm, 2), "a3"), (A4, blk(T.xm, 1), "a45"), (A5, blk(T.xm, 0), "a45")]
+        for i, (pw, src, item) in enumerate(terms):
+            ready(PE, "pe", item)
+            if not (p == 0 and i == 0):
+                wait(PE, "pe", "mx", nx)
+            PE.matmul(blk(T.pd, 0), blk(T.w, pw), src, start=(i == 0), stop=(i == 2)).then_inc(T.sem.dm, 1)
+    if p == 1:
+        wait(PE, "pe", "c", 1)
+        wait(PE, "pe", "mx", nx)
+        ready(PE, "pe", "a2")
+        PE.matmul(blk(T.pc, 2), blk(T.w, A1), blk(T.xm, 1), start=True, stop=False).then_inc(T.sem.cm, 1)
+        PE.matmul(blk(T.pc, 2), blk(T.w, A2), blk(T.xm, 0), start=False, stop=True).then_inc(T.sem.cm, 1)
+    for j in late:
+        job_pe(j)
     py = [T.py0, T.py1, T.py2]
-    for j, (slot, m, ne) in enumerate(msgs):
-        wait(PE, "pe", "m%d" % slot, ne)
+    for j, (src, m, sem, cnt) in enumerate(msgs):
+        wait(PE, "pe", sem, cnt)
+        for it in _tri_items(m):
+            ready(PE, "pe", it)
         for s in range(S):
-            ready(PE, "pe", ("a", "a2", "a3")[s] if m == 0 else "t%d" % m)
-            PE.matmul(blk(py[s], 0), blk(T.w, TRI[m] + s), blk(T.land, slot),
+            PE.matmul(blk(py[s], 0), blk(T.w, TRI[m] + s), src,
                       start=(j == 0), stop=(j == len(msgs) - 1)).then_inc(T.sem["y%d" % s], 1)
 
     wait(V, "v", "ldx", 16)
@@ -203,19 +240,25 @@ def rank_program(g, core, T, topo):
     V.tensor_tensor(blk(T.lc, 0), blk(T.pc, 0), blk(T.xs, 1), op=AluOpType.add).then_inc(T.sem.l1, 1)
     wait(V, "v", "mm2", 1)
     V.tensor_tensor(blk(T.lc, 1), blk(T.pc, 1), blk(T.xs, 2), op=AluOpType.add).then_inc(T.sem.c, 1)
-    for i in early:
-        job_v(i)
+    for j in early:
+        if j[1] == "v":
+            job_copy(j)
     if make_d:
-        wait(V, "v", "dm", 1)
+        wait(V, "v", "dm", 3)
         if p == 0:
-            wait(V, "v", "m%d" % (r + 1), _bits(swap_mask(r + 1)))
-            second = blk(T.land, r + 1)
+            wait(V, "v", "mx", nx)
+            rest = blk(T.xm, 2)
         else:
             wait(V, "v", "c", 1)
-            second = blk(T.lc, 1)
-        V.tensor_tensor(T.dd[:, :], blk(T.pc, 2), second, op=AluOpType.add).then_inc(T.sem.d, 1)
-    for i in late:
-        job_v(i)
+            rest = blk(T.lc, 1)
+        V.tensor_tensor(T.dd[:, :], blk(T.pd, 0), rest, op=AluOpType.add).then_inc(T.sem.d, 1)
+    if p == 1:
+        wait(V, "v", "cm", 2)
+        wait(V, "v", "mx", nx)
+        V.tensor_tensor(T.cf[:, :], blk(T.pc, 2), blk(T.xm, 2), op=AluOpType.add).then_inc(T.sem.cfs, 1)
+    for j in late:
+        if j[1] == "v":
+            job_copy(j)
     if msgs:
         wait(V, "v", "l1", 1)
         wait(V, "v", "c", 1)
@@ -224,36 +267,36 @@ def rank_program(g, core, T, topo):
             wait(V, "v", "y%d" % s, len(msgs))
             V.tensor_tensor(blk(T.ys, s), blk(py[s], 0), loc[s], op=AluOpType.add).then_inc(T.sem.fin, 1)
 
+    for j in jobs:
+        if j[1] == "s":
+            job_copy(j)
+
     sent = [0]
 
-    def send(src, slot, dests, mask):
+    def send(src, dst, sem, dests, mask):
         for o in dests:
             if not topo.may_write(core, cores[o]):
                 raise ValueError("rank %d may not write to rank %d" % (r, o))
         ids = [topo.addr(cores[o]) for o in dests]
         if len(dests) == 1:
-            g.remote_dma(out_ap=blk(T.land, slot), in_ap=src, remote_sem=T.sem["m%d" % slot], local_sem=T.sem.sent,
+            g.remote_dma(out_ap=dst, in_ap=src, remote_sem=T.sem[sem], local_sem=T.sem.sent,
                          pid=ids[0][1], routing_id=ids[0][0], dma_engine_mask=mask)
         else:
             g.remote_dma_fused([RemoteDMATransfer(dst_ids=[DstId(rid=a[0], pnc=a[1]) for a in ids], dma_engine_mask=mask,
-                                                  remote_sem=T.sem["m%d" % slot], srcs=[src],
-                                                  dsts=[blk(T.land, slot) for _ in ids], alu_op=0)], local_sem=T.sem.sent)
+                                                  remote_sem=T.sem[sem], srcs=[src],
+                                                  dsts=[dst for _ in ids], alu_op=0)], local_sem=T.sem.sent)
         sent[0] += _bits(mask)
 
     direct = [o for m in direct_groups(k) for o in groups[m]]
-    swap = p == 0 or make_d
-    mate = [o for o in groups[k] if o != r][0]
-    if swap or direct:
-        wait(g, "g", "c", 1)
-    if swap and make_d:
-        send(blk(T.lc, 1), r, [mate], swap_mask(r))
+    if send_x:
+        wait(g, "g", "ldx", 16)
+        send(T.xs[:, :], T.xm[:, :], "mx", [mate], topo.mask(core, cores[mate]))
     if direct:
-        send(blk(T.lc, 1), r, direct, off_mask(r))
-    if swap and not make_d:
-        send(blk(T.lc, 1), r, [mate], swap_mask(r))
+        wait(g, "g", "c", 1)
+        send(blk(T.lc, 1), blk(T.land, r), "m%d" % r, direct, off_mask(r))
     if make_d:
         wait(g, "g", "d", 1)
-        send(T.dd[:, :], N - 1 + k, [groups[m][p] for m in comb_groups(k)], off_mask(r))
+        send(T.dd[:, :], blk(T.land, N - 1 + k), "m%d" % (N - 1 + k), [groups[m][p] for m in comb_groups(k)], off_mask(r))
     if sent[0]:
         wait(g, "g", "sent", sent[0])
 

from concourse.bass import DstId, RemoteDMATransfer
from concourse.mybir import AluOpType, ActivationFunctionType

N, S, B = 8, 3, 128
SPAN = 1
NSLOT = N - 1 + N // 2 - 1

AT, A1, A2, A3, A4, A5, A6, Q6, Q3, Q12 = 0, 1, 2, 3, 4, 5, 6, 7, 8, 12
TRI = [1, 4, 9, 13, 16, 19]
NW = 22
JOBS = [
    ("j1", "s", [("a2", 2, 1, AT, A1)]),
    ("j2q", "s", [("q3", 8, 1, A2, AT)]),
    ("j2a", "v", [("a3", 3, 1, AT, A2)]),
    ("j3a", "s", [("a45", 4, 2, Q3, A1)]),
    ("j3b", "v", [("a6", 6, 1, Q3, A3), ("q6", 7, 1, A3, Q3)]),
    ("j4a", "s", [("t2", 9, 3, Q6, A1), ("q12", 12, 1, A6, Q6)]),
    ("j4b", "v", [("t3", 13, 3, Q6, A4)]),
    ("j5a", "v", [("t4", 16, 3, Q12, A1)]),
    ("j5b", "s", [("t5", 19, 3, Q12, A4)]),
]
DEPS = {"a": [], "at": [], "a2": ["a", "at"], "a3": ["at", "a2"], "q3": ["a2", "at"], "a45": ["q3", "a", "a2"],
        "a6": ["q3", "a3"], "q6": ["a3", "q3"], "t2": ["q6", "a", "a2", "a3"], "q12": ["a6", "q6"],
        "t3": ["q6", "a45", "a6"], "t4": ["q12", "a", "a2", "a3"], "t5": ["q12", "a45", "a6"]}
ITEM_JOB = {}
for _j, _e, _parts in JOBS:
    for _p in _parts:
        ITEM_JOB[_p[0]] = _j

SCRATCH = {
    "xs": ("sbuf", [128, S * B], "bfloat16"),
    "xm": ("sbuf", [128, S * B], "bfloat16"),
    "w": ("sbuf", [128, NW * B], "bfloat16"),
    "lc": ("sbuf", [128, 2 * B], "bfloat16"),
    "cf": ("sbuf", [128, B], "bfloat16"),
    "dd": ("sbuf", [128, B], "bfloat16"),
    "land": ("sbuf", [128, NSLOT * B], "bfloat16"),
    "ys": ("sbuf", [128, S * B], "bfloat16"),
    "pc": ("psum", [128, 512], "float32"),
    "pd": ("psum", [128, 512], "float32"),
    "py0": ("psum", [128, 512], "float32"),
    "py1": ("psum", [128, 512], "float32"),
    "py2": ("psum", [128, 512], "float32"),
    "pp0": ("psum", [128, 512], "float32"),
    "pp1": ("psum", [128, 512], "float32"),
    "pp2": ("psum", [128, 512], "float32"),
}
SEMAPHORES = (["ldx", "lda", "ldat", "mm1", "l1", "mm2", "c", "dm", "d", "cm", "cfs", "mx", "y0", "y1", "y2", "fin", "st",
               "sent"]
              + ["m%d" % i for i in range(NSLOT)]
              + ["t" + j[0] for j in JOBS] + ["v" + j[0] for j in JOBS])


def _bits(m):
    return bin(m).count("1")


def _tri_items(m):
    if m == 0:
        return ["a", "a2", "a3"]
    if m == 1:
        return ["a45", "a6"]
    return ["t%d" % m]


def rank_program(g, core, T, topo):
    r = T.rank_of(core)
    if r is None:
        return
    cores = list(T.cores)
    groups = []
    for i, c in enumerate(cores):
        if groups and topo.chip(cores[groups[-1][0]]) == topo.chip(c):
            groups[-1].append(i)
        else:
            groups.append([i])
    G = len(groups)
    grp = {q: k for k, m in enumerate(groups) for q in m}
    k = grp[r]
    p = groups[k].index(r)
    PE, V, SY, SC = g.tensor, g.vector, g.sync, g.scalar

    def direct_groups(kk):
        return [m for m in range(kk + 1, G) if m - kk <= SPAN]

    def comb_groups(kk):
        return [m for m in range(kk + 1, G) if m - kk > SPAN]

    def off_mask(q):
        m = None
        for o in range(N):
            if grp[o] != grp[q]:
                mm = topo.mask(cores[q], cores[o])
                m = mm if m is None else (m & mm)
        return m

    seen = {}

    def wait(q, qn, sem, val):
        if seen.get((qn, sem), 0) >= val:
            return
        seen[(qn, sem)] = val
        q.wait_ge(T.sem[sem], val)

    def ready(q, qn, item):
        if item == "a":
            wait(q, qn, "lda", 16)
        elif item == "at":
            wait(q, qn, "ldat", 16)
        else:
            wait(q, qn, "v" + ITEM_JOB[item], 1)

    def blk(t, i, n=1):
        return t[:, i * B:(i + n) * B]

    mate = [o for o in groups[k] if o != r][0]
    make_d = bool(comb_groups(k))
    send_x = p == 0 or make_d
    recv_x = p == 1 or make_d
    nx = _bits(topo.mask(cores[mate], core))

    msgs = []
    if p == 1:
        msgs.append((T.cf[:, :], 0, "cfs", 1))
    for kk in range(k - 1, -1, -1):
        if k - kk <= SPAN:
            for q in reversed(groups[kk]):
                msgs.append((blk(T.land, q), r - q - 1, "m%d" % q, _bits(off_mask(q))))
    for kk in range(k - 1, -1, -1):
        if k - kk > SPAN:
            msgs.append((blk(T.land, N - 1 + kk), r - groups[kk][-1] - 1, "m%d" % (N - 1 + kk),
                         _bits(off_mask(groups[kk][p]))))

    def closure(items):
        out = set()

        def want(item):
            if item in out:
                return
            out.add(item)
            for d in DEPS[item]:
                want(d)
        for it in items:
            want(it)
        return out

    dneed = []
    if make_d:
        dneed = ["a", "a2", "a3"] if p == 0 else ["a3", "a45"]
    wanted = ["a"] + dneed
    if p == 1:
        wanted += ["a", "a2"]
    for _src, m, _s, _n in msgs:
        wanted += _tri_items(m)
    need = closure(wanted)
    first = closure(dneed) if make_d else need
    early, late = [], []
    for name, eng, parts in JOBS:
        ps = [q for q in parts if q[0] in need]
        if not ps:
            continue
        if any(q[0] in first for q in ps):
            early.append((name, eng, ps))
        else:
            late.append((name, eng, ps))
    jobs = early + late
    pos = {j[0]: i for i, j in enumerate(jobs)}

    SY.dma_start(T.xs[:, :], T.x[:, :]).then_inc(T.sem.ldx, 16)
    SC.dma_start(blk(T.w, A1), T.a[:, :]).then_inc(T.sem.lda, 16)
    if "at" in need:
        SC.dma_start(blk(T.w, AT), T.at[:, :]).then_inc(T.sem.ldat, 16)

    banks = [T.pp0, T.pp1, T.pp2]

    def job_pe(job):
        name, _eng, ps = job
        i = pos[name]
        if i >= len(banks):
            wait(PE, "pe", "v" + jobs[i - len(banks)][0], 1)
        col = 0
        for item, _o, n, lh, rh in ps:
            for d in DEPS[item]:
                ready(PE, "pe", d)
            PE.matmul(banks[i % len(banks)][:, col * B:(col + n) * B], blk(T.w, lh), blk(T.w, rh, n),
                      start=True, stop=True).then_inc(T.sem["t" + name], 1)
            col += n

    def job_copy(job):
        name, eng, ps = job
        i = pos[name]
        n = sum(q[2] for q in ps)
        out, src = blk(T.w, ps[0][1], n), banks[i % len(banks)][:, 0:n * B]
        if eng == "v":
            wait(V, "v", "t" + name, len(ps))
            V.tensor_copy(out, src).then_inc(T.sem["v" + name], 1)
        else:
            wait(SC, "sc", "t" + name, len(ps))
            SC.activation(out, src, ActivationFunctionType.Copy).then_inc(T.sem["v" + name], 1)

    wait(PE, "pe", "lda", 16)
    wait(PE, "pe", "ldx", 16)
    PE.matmul(blk(T.pc, 0), blk(T.w, A1), blk(T.xs, 0), start=True, stop=True).then_inc(T.sem.mm1, 1)
    if early:
        job_pe(early[0])
    wait(PE, "pe", "l1", 1)
    PE.matmul(blk(T.pc, 1), blk(T.w, A1), blk(T.lc, 0), start=True, stop=True).then_inc(T.sem.mm2, 1)
    for j in early[1:]:
        job_pe(j)
    if make_d:
        if p == 0:
            terms = [(A3, blk(T.lc, 1), "a3"), (A1, blk(T.xm, 1), "a"), (A2, blk(T.xm, 0), "a2")]
            wait(PE, "pe", "c", 1)
        else:
            terms = [(A3, blk(T.xm, 2), "a3"), (A4, blk(T.xm, 1), "a45"), (A5, blk(T.xm, 0), "a45")]
        for i, (pw, src, item) in enumerate(terms):
            ready(PE, "pe", item)
            if not (p == 0 and i == 0):
                wait(PE, "pe", "mx", nx)
            PE.matmul(blk(T.pd, 0), blk(T.w, pw), src, start=(i == 0), stop=(i == 2)).then_inc(T.sem.dm, 1)
    if p == 1:
        wait(PE, "pe", "c", 1)
        wait(PE, "pe", "mx", nx)
        ready(PE, "pe", "a2")
        PE.matmul(blk(T.pc, 2), blk(T.w, A1), blk(T.xm, 1), start=True, stop=False).then_inc(T.sem.cm, 1)
        PE.matmul(blk(T.pc, 2), blk(T.w, A2), blk(T.xm, 0), start=False, stop=True).then_inc(T.sem.cm, 1)
    for j in late:
        job_pe(j)
    py = [T.py0, T.py1, T.py2]
    for j, (src, m, sem, cnt) in enumerate(msgs):
        wait(PE, "pe", sem, cnt)
        for it in _tri_items(m):
            ready(PE, "pe", it)
        for s in range(S):
            PE.matmul(blk(py[s], 0), blk(T.w, TRI[m] + s), src,
                      start=(j == 0), stop=(j == len(msgs) - 1)).then_inc(T.sem["y%d" % s], 1)

    wait(V, "v", "ldx", 16)
    wait(V, "v", "mm1", 1)
    V.tensor_tensor(blk(T.lc, 0), blk(T.pc, 0), blk(T.xs, 1), op=AluOpType.add).then_inc(T.sem.l1, 1)
    wait(V, "v", "mm2", 1)
    V.tensor_tensor(blk(T.lc, 1), blk(T.pc, 1), blk(T.xs, 2), op=AluOpType.add).then_inc(T.sem.c, 1)
    for j in early:
        if j[1] == "v":
            job_copy(j)
    if make_d:
        wait(V, "v", "dm", 3)
        if p == 0:
            wait(V, "v", "mx", nx)
            rest = blk(T.xm, 2)
        else:
            wait(V, "v", "c", 1)
            rest = blk(T.lc, 1)
        V.tensor_tensor(T.dd[:, :], blk(T.pd, 0), rest, op=AluOpType.add).then_inc(T.sem.d, 1)
    if p == 1:
        wait(V, "v", "cm", 2)
        wait(V, "v", "mx", nx)
        V.tensor_tensor(T.cf[:, :], blk(T.pc, 2), blk(T.xm, 2), op=AluOpType.add).then_inc(T.sem.cfs, 1)
    for j in late:
        if j[1] == "v":
            job_copy(j)
    if msgs:
        wait(V, "v", "l1", 1)
        wait(V, "v", "c", 1)
        loc = [blk(T.xs, 0), blk(T.lc, 0), blk(T.lc, 1)]
        for s in range(S):
            wait(V, "v", "y%d" % s, len(msgs))
            V.tensor_tensor(blk(T.ys, s), blk(py[s], 0), loc[s], op=AluOpType.add).then_inc(T.sem.fin, 1)

    for j in jobs:
        if j[1] == "s":
            job_copy(j)

    sent = [0]

    def send(src, dst, sem, dests, mask):
        for o in dests:
            if not topo.may_write(core, cores[o]):
                raise ValueError("rank %d may not write to rank %d" % (r, o))
        ids = [topo.addr(cores[o]) for o in dests]
        if len(dests) == 1:
            g.remote_dma(out_ap=dst, in_ap=src, remote_sem=T.sem[sem], local_sem=T.sem.sent,
                         pid=ids[0][1], routing_id=ids[0][0], dma_engine_mask=mask)
        else:
            g.remote_dma_fused([RemoteDMATransfer(dst_ids=[DstId(rid=a[0], pnc=a[1]) for a in ids], dma_engine_mask=mask,
                                                  remote_sem=T.sem[sem], srcs=[src],
                                                  dsts=[dst for _ in ids], alu_op=0)], local_sem=T.sem.sent)
        sent[0] += _bits(mask)

    direct = [o for m in direct_groups(k) for o in groups[m]]
    if send_x:
        wait(g, "g", "ldx", 16)
        send(T.xs[:, :], T.xm[:, :], "mx", [mate], topo.mask(core, cores[mate]))
    if direct:
        wait(g, "g", "c", 1)
        send(blk(T.lc, 1), blk(T.land, r), "m%d" % r, direct, off_mask(r))
    if make_d:
        wait(g, "g", "d", 1)
        send(T.dd[:, :], blk(T.land, N - 1 + k), "m%d" % (N - 1 + k), [groups[m][p] for m in comb_groups(k)], off_mask(r))
    if sent[0]:
        wait(g, "g", "sent", sent[0])

    if msgs:
        wait(SY, "sy", "fin", S)
        SY.dma_start(T.y[:, :], T.ys[:, :]).then_inc(T.sem.st, 16)
        wait(SY, "sy", "st", 16)
    else:
        wait(SY, "sy", "ldx", 16)
        SY.dma_start(T.y[:, 0:B], blk(T.xs, 0)).then_inc(T.sem.st, 16)
        wait(SY, "sy", "l1", 1)
        wait(SY, "sy", "c", 1)
        SY.dma_start(T.y[:, B:S * B], T.lc[:, :]).then_inc(T.sem.st, 16)
        wait(SY, "sy", "st", 32)
